import numpy as np
import ml_dtypes


def mxq(x, axis, fmt="e4m3"):
    dtype, down = {"e4m3": (ml_dtypes.float8_e4m3fn, 7), "e5m2": (ml_dtypes.float8_e5m2, 14)}[fmt]
    v = np.moveaxis(np.asarray(x, np.float32).astype(ml_dtypes.bfloat16).astype(np.float64), axis, -1)
    blocks = v.reshape(v.shape[:-1] + (-1, 32))
    amax = np.abs(blocks).max(-1, keepdims=True)
    byte = np.maximum(np.where(amax > 0, np.frexp(amax)[1] - 1 + 127, 0) - down, 1)
    scale = np.exp2(byte - 127.0)
    codes = (blocks / scale).astype(np.float32).astype(dtype).astype(np.float64)
    return np.moveaxis((codes * scale).reshape(v.shape), -1, axis)


WIDE = False


def mx_kscale(k):
    if not WIDE:
        return np.ones(k)
    levels = np.array([10, -10, 5, -5, 0])
    if k % 512:
        return np.exp2(np.random.permutation(np.resize(levels, k // 32))).repeat(32)
    a = np.empty((k // 512, 16))
    for p in range(k // 512):
        a[p, :8] = np.random.permutation(np.resize(levels, 8))
        for g in range(8):
            far = levels[np.abs(levels - a[p, g]) >= 10]
            a[p, g + 8] = far[np.random.randint(len(far))]
    return np.exp2(a.ravel()).repeat(32)


def f64(x):
    return np.asarray(x).astype(np.float64)


def striped(idx):
    return np.tile(idx.reshape(-1, 16).T, (8, 1)).astype(np.uint16)


def unstriped(offs):
    return offs[:16].T.reshape(-1).astype(np.int64)


E2M1 = np.array([0.0, 0.5, 1.0, 1.5, 2.0, 3.0, 4.0, 6.0, -0.0, -0.5, -1.0, -1.5, -2.0, -3.0, -4.0, -6.0])


def pack_weight(w, fmt):
    k, n = w.shape
    w = f64(np.asarray(w, np.float32).astype(ml_dtypes.bfloat16)).reshape(k // 32, 32, n)
    amax = np.abs(w).max(1)
    if fmt == "e4m3":
        byte = np.frexp(amax)[1] - 1 + 127 - 7
    else:
        mant, ex = np.frexp(amax / 6.0)
        byte = np.where(mant > 0.5, ex, ex - 1) + 127
    byte = np.clip(np.where(amax > 0, byte, 1), 1, 254)
    scaled = (w * np.exp2(127.0 - byte)[:, None, :]).reshape(k, n).astype(np.float32)
    by_word = np.ascontiguousarray(scaled.reshape(k // 512, 128, 4, n).transpose(0, 1, 3, 2))
    if fmt == "e4m3":
        words = by_word.astype(ml_dtypes.float8_e4m3fn).view(np.uint8)
    else:
        c = by_word.astype(ml_dtypes.float4_e2m1fn).view(np.uint8) & 0xF
        words = (c[..., 0::2] | (c[..., 1::2] << 4)).reshape(k // 512, 128, 2 * n)
    return np.ascontiguousarray(words), np.ascontiguousarray(byte.astype(np.uint8).reshape(k // 512, 16, n))


def unpack_weight(words, scales, fmt):
    g, _, n = scales.shape
    words = np.ascontiguousarray(words).reshape(g, 128, n, -1)
    if fmt == "e4m3":
        vals = words.view(ml_dtypes.float8_e4m3fn).astype(np.float64)
    else:
        nib = np.empty((g, 128, n, 4), np.uint8)
        nib[..., 0::2] = words & 0xF
        nib[..., 1::2] = words >> 4
        vals = E2M1[nib]
    vals = vals * np.repeat(np.exp2(scales.astype(np.float64) - 127.0), 8, axis=1)[..., None]
    return vals.transpose(0, 1, 3, 2).reshape(g * 512, n)


def gelu(v):
    return 0.5 * v * (1.0 + np.tanh(np.sqrt(2.0 / np.pi) * (v + 0.044715 * v**3)))


K, KB, H, N, T, S, P, T2 = 1024, 512, 1024, 384, 2048, 1024, 512, 2048

def setup_inputs():
    n = np.random.standard_normal
    s, sb, u = mx_kscale(K)[:, None], mx_kscale(KB)[:, None], mx_kscale(H)[:, None]
    tab_words, tab_scales = pack_weight(n((K, T)) * s, "e4m3")
    tab2_words, tab2_scales = pack_weight(n((KB, T)) * sb, "e4m3")
    w1_words, w1_scales = pack_weight(1.5 * n((K, H)) / s / np.sqrt(K), "e2m1")
    w4_words, w4_scales = pack_weight(1.3 * n((H, N)) / u ** 2 / np.sqrt(H), "e4m3")
    perm = np.random.permutation(T2)
    return {
        "tab_words": tab_words, "tab_scales": tab_scales,
        "tab2_words": tab2_words, "tab2_scales": tab2_scales,
        "w1_words": w1_words, "w1_scales": w1_scales,
        "gain": (np.random.uniform(0.6, 1.8, H) * u[:, 0]).astype(np.float32),
        "w2": (n((KB, H)) / sb * u.T / np.sqrt(KB)).astype(np.float32),
        "w3": (1.2 * n((H, N)) / u / np.sqrt(H)).astype(np.float32),
        "d": (0.8 * n(N)).astype(np.float32),
        "w4_words": w4_words, "w4_scales": w4_scales,
        "page1": n((N, T2)).astype(np.float32),
        "wg1": np.exp(0.3 * n((128, S))).astype(np.float32),
        "wg2": np.exp(0.3 * n((128, P))).astype(np.float32),
        "offs": striped(np.random.permutation(T)[:S]),
        "offs2": striped(np.random.permutation(T)[:P]),
        "pos1": striped(np.random.permutation(S)[:P]),
        "offs3": striped(perm[:S]), "offs4": striped(perm[S:S + P])}

def reference(tab_words, tab_scales, tab2_words, tab2_scales, w1_words, w1_scales, gain, w2, w3, d,
              w4_words, w4_scales, page1, wg1, wg2, offs, offs2, pos1, offs3, offs4):
    v = unpack_weight(tab_words, tab_scales, "e4m3")[:, unstriped(offs)]
    v2 = unpack_weight(tab2_words, tab2_scales, "e4m3")[:, unstriped(offs2)]
    w1 = unpack_weight(w1_words, w1_scales, "e2m1")
    w4 = unpack_weight(w4_words, w4_scales, "e4m3")
    h1 = f64(gain)[:, None] * np.tanh(w1.T @ v)
    h2 = mxq(f64(w2), 0, "e4m3").T @ v2
    top = h1[:, unstriped(pos1)]
    z2 = (h2 - top) * top
    y1 = (mxq(f64(w3), 0, "e4m3").T @ mxq(h1, 0, "e4m3")) + f64(d)[:, None]
    y2 = w4.T @ mxq(z2, 0, "e4m3")
    out = f64(page1).copy()
    out[:, unstriped(offs3)] = np.tile(f64(wg1), (N // 128, 1)) * y1
    out[:, unstriped(offs4)] = np.tile(f64(wg2), (N // 128, 1)) * y2
    return out

@@ -1,0 +1,262 @@
+from contextlib import ExitStack
+
+import concourse.mybir as mybir
+
+K, KB, H, N, T, S, PC, T2 = 1024, 512, 1024, 384, 2048, 1024, 512, 2048
+FLOPS = 2 * (K * H * S + KB * H * PC + H * N * S + H * N * PC)
+
+F32 = mybir.dt.float32
+BF16 = mybir.dt.bfloat16
+I32 = mybir.dt.int32
+U32 = mybir.dt.uint32
+U16 = mybir.dt.uint16
+U8 = mybir.dt.uint8
+FP8X4 = mybir.dt.float8_e4m3fn_x4
+FP4X4 = mybir.dt.float4_e2m1fn_x4
+ACT = mybir.ActivationFunctionType
+ALU = mybir.AluOpType
+
+P = 128
+PACK = 4
+KP = P * PACK
+COLS = 512
+
+
+def tile_list_repair_estimate_features_kernel(
+    tc, tab_words, tab_scales, tab2_words, tab2_scales, w1_words, w1_scales, gain, w2, w3, d,
+    w4_words, w4_scales, page1, wg1, wg2, offs, offs2, pos1, offs3, offs4, out,
+):
+    nc = tc.nc
+    with ExitStack() as ctx:
+        keep = ctx.enter_context(tc.tile_pool(name="keep", bufs=1))
+        ring = ctx.enter_context(tc.tile_pool(name="ring", bufs=3))
+        weave = ctx.enter_context(tc.tile_pool(name="weave", bufs=4))
+        ps1 = ctx.enter_context(tc.psum_pool(name="ps1", bufs=2))
+        ps2 = ctx.enter_context(tc.psum_pool(name="ps2", bufs=2))
+        ps3 = ctx.enter_context(tc.psum_pool(name="ps3", bufs=2))
+
+        def held(name, shape, dtype, tag=None):
+            return keep.tile(shape, dtype, name=name, tag=tag or name, align_bytes=64)
+
+        def woven(name, width):
+            return weave.tile([P, PACK * width], BF16, name=name, tag="woven", align_bytes=64)
+
+        def load_list(name, src):
+            t = keep.tile(list(src.shape), U16, name=name)
+            nc.sync.dma_start(t[:], src)
+            return t
+
+        def zeroed(name, shape):
+            t = held(name, shape, U8)
+            nc.vector.memset(t[:].bitcast(I32), 0)
+            return t
+
+        tab_s = zeroed("tab_s", [P, T])
+        w1_s = zeroed("w1_s", [P, 2, H])
+        tab2_s = zeroed("tab2_s", [P, T])
+        v_s1 = zeroed("v_s1", [P, S])
+        w4_s = zeroed("w4_s", [P, 2, N])
+
+        l_offs = load_list("l_offs", offs)
+        for q in range(4):
+            nc.sync.dma_start(tab_s[32 * q : 32 * q + 8, :].bitcast(I32), tab_scales[:, 4 * q : 4 * q + 4, :].bitcast(I32))
+        for q in range(4):
+            nc.sync.dma_start(
+                w1_s[32 * q : 32 * q + 4, :, :].bitcast(I32),
+                w1_scales[:, 4 * q : 4 * q + 4, :].rearrange("a r c -> r a c").bitcast(I32),
+            )
+        w1_w = held("w1_w", [P, 2, 2 * H], U8)
+        nc.sync.dma_start(w1_w[:].bitcast(I32), w1_words.rearrange("a p c -> p a c").bitcast(I32))
+        tab_w = []
+        for a in range(2):
+            t = held("tab_w%d" % a, [P, T], U32)
+            nc.sync.dma_start(t[:].bitcast(I32), tab_words[a].rearrange("p t i -> p (t i)").bitcast(I32))
+            tab_w.append(t)
+        w2_rows = w2.rearrange("(p j) c -> p j c", j=PACK)
+        w2_raw = [held("w2_raw%d" % b, [P, PACK, KP], F32) for b in range(2)]
+        nc.sync.dma_start(w2_raw[0][:], w2_rows[:, :, 0:KP])
+        gain_t = held("gain_t", [P, 2, PACK], F32)
+        nc.sync.dma_start(gain_t[:], gain.rearrange("(b p t) -> p b t", b=2, t=PACK))
+        l_offs2 = load_list("l_offs2", offs2)
+        l_pos1 = load_list("l_pos1", pos1)
+        for q in range(4):
+            nc.sync.dma_start(tab2_s[32 * q : 32 * q + 4, :].bitcast(I32), tab2_scales[0, 4 * q : 4 * q + 4, :].bitcast(I32))
+        tab2_w = held("tab2_w", [P, T], U32)
+        nc.sync.dma_start(tab2_w[:].bitcast(I32), tab2_words[0].rearrange("p t i -> p (t i)").bitcast(I32))
+        nc.sync.dma_start(w2_raw[1][:], w2_rows[:, :, KP : 2 * KP])
+        w4_w = held("w4_w", [P, 2, N], U32)
+        nc.sync.dma_start(w4_w[:].bitcast(I32), w4_words.rearrange("a p c i -> p a (c i)").bitcast(I32))
+        for q in range(4):
+            nc.sync.dma_start(
+                w4_s[32 * q : 32 * q + 4, :, :].bitcast(I32),
+                w4_scales[:, 4 * q : 4 * q + 4, :].rearrange("a r c -> r a c").bitcast(I32),
+            )
+        w3_raw = []
+        for b in range(2):
+            t = held("w3_raw%d" % b, [P, PACK, N], F32)
+            nc.sync.dma_start(t[:], w3[b * KP : (b + 1) * KP, :].rearrange("(p j) n -> p j n", j=PACK))
+            w3_raw.append(t)
+        l_offs4 = load_list("l_offs4", offs4)
+        l_offs3 = load_list("l_offs3", offs3)
+        wg2_t = held("wg2_t", [P, PC], F32)
+        nc.sync.dma_start(wg2_t[:], wg2)
+        pages = []
+        for c in range(3):
+            t = held("page%d" % c, [P, T2], F32)
+            nc.sync.dma_start(t[:], page1[c * P : (c + 1) * P, :])
+            pages.append(t)
+        wg1_t = held("wg1_t", [P, S], F32)
+        nc.sync.dma_start(wg1_t[:], wg1)
+        d_t = held("d_t", [P, 3], F32)
+        with nc.allow_non_contiguous_dma(reason="one bias value for each partition"):
+            nc.sync.dma_start(d_t[:], d.rearrange("(c p) -> p c", p=P))
+
+        v_s0 = held("v_s0", [P, S], U8)
+        nc.vector.tensor_copy(v_s0[:], tab_s[:].indirect(l_offs[:]))
+        for q in range(4):
+            nc.scalar.dma_start(v_s1[32 * q : 32 * q + 4, :].bitcast(I32), v_s0[32 * q + 4 : 32 * q + 8, :].bitcast(I32))
+        v_s = [v_s0, v_s1]
+        w1_sd = held("w1_sd", [P, 2, H], U8)
+        nc.vector.tensor_copy(
+            w1_sd[:].rearrange("p a (b t m) -> p (a b) t m", b=2, t=PACK),
+            w1_s[:].rearrange("p a (b m t) -> p (a b) t m", b=2, t=PACK),
+        )
+        w1_wd = held("w1_wd", [P, 2, 2 * H], U8)
+        nc.vector.tensor_copy(
+            w1_wd[:].bitcast(U16).rearrange("p a (b t m) -> p (a b) t m", b=2, t=PACK),
+            w1_w[:].bitcast(U16).rearrange("p a (b m t) -> p (a b) t m", b=2, t=PACK),
+        )
+        v_w = []
+        for hf in range(2):
+            row = []
+            for a in range(2):
+                t = held("v_w%d%d" % (hf, a), [P, COLS], U32)
+                nc.vector.tensor_copy(t[:], tab_w[a][:].indirect(l_offs[:, 32 * hf : 32 * (hf + 1)]))
+                row.append(t)
+            v_w.append(row)
+        v2_s = held("v2_s", [P, PC], U8)
+        nc.vector.tensor_copy(v2_s[:], tab2_s[:].indirect(l_offs2[:]))
+        v2_w = held("v2_w", [P, PC], U32)
+        nc.vector.tensor_copy(v2_w[:], tab2_w[:].indirect(l_offs2[:]))
+
+        def quantise(name, src, width):
+            codes = held(name + "_w", [P, width], U32)
+            scales = held(name + "_s", [P, width], U8)
+            nc.vector.quantize_mx(out=codes[:].bitcast(FP8X4), scales=scales[:], in_=src[:])
+            return codes, scales
+
+        def round_w2(b):
+            g = woven("w2_g%d" % b, KP)
+            nc.scalar.copy(
+                g[:].rearrange("p (t m j) -> p m j t", t=PACK, j=PACK),
+                w2_raw[b][:].rearrange("p j (m t) -> p m j t", t=PACK),
+            )
+            return quantise("w2q%d" % b, g, KP)
+
+        def weave_out(ap):
+            return ap.rearrange("p (c i t) -> p c t i", i=4, t=PACK)
+
+        def weave_in(ap):
+            return ap.rearrange("p t (c i) -> p c t i", i=4)
+
+        h1 = [held("h1_%d" % b, [P, PACK, S], F32) for b in range(2)]
+        top = [held("top%d" % b, [P, PACK, PC], F32) for b in range(2)]
+        dif = [held("dif%d" % b, [P, PACK, PC], F32, tag="tab_w%d" % b) for b in range(2)]
+        w2q = [round_w2(0)]
+
+        def line_features(b, t):
+            th = ring.tile([P, S], F32, name="th")
+            c0 = b * KP + t * P
+            for hf in range(2):
+                cols = slice(hf * COLS, (hf + 1) * COLS)
+                acc = ps1.tile([P, COLS], F32, name="acc1_%d" % hf)
+                for a in range(2):
+                    nc.tensor.matmul_mx(
+                        out=acc[:],
+                        lhsT=w1_wd[:, a, 2 * c0 : 2 * (c0 + P)].bitcast(FP4X4),
+                        lhsT_scale=w1_sd[:, a, c0 : c0 + P],
+                        rhs=v_w[hf][a][:].bitcast(FP8X4),
+                        rhs_scale=v_s[a][:, cols],
+                        start=(a == 0),
+                        stop=(a == 1),
+                    )
+                nc.scalar.activation(th[:, cols], acc[:], ACT.Tanh)
+            nc.scalar.activation(h1[b][:, t, :], th[:], ACT.Copy, scale=gain_t[:, b, t : t + 1])
+
+        def claim_difference(b, t):
+            acc = ps2.tile([P, PC], F32, name="acc2")
+            nc.tensor.matmul_mx(
+                out=acc[:],
+                lhsT=w2q[b][0][:, t * P : (t + 1) * P].bitcast(FP8X4),
+                lhsT_scale=w2q[b][1][:, t * P : (t + 1) * P],
+                rhs=v2_w[:].bitcast(FP8X4),
+                rhs_scale=v2_s[:],
+                start=True,
+                stop=True,
+            )
+            nc.vector.tensor_copy(top[b][:, t, :], h1[b][:, t, :].indirect(l_pos1[:]))
+            nc.vector.tensor_tensor(dif[b][:, t, :], acc[:], top[b][:, t, :], ALU.subtract)
+
+        def claim_product(b, hf):
+            g = woven("z_g%d%d" % (b, hf), PC // 2)
+            cols = slice(hf * PC // 2, (hf + 1) * PC // 2)
+            nc.vector.tensor_tensor(weave_out(g[:]), weave_in(dif[b][:, :, cols]), weave_in(top[b][:, :, cols]), ALU.mult)
+            return g
+
+        zq = [[], []]
+        for b in range(2):
+            for t in range(PACK):
+                line_features(b, t)
+                claim_difference(b, t)
+                if b == 0 and t == 1:
+                    w2q.append(round_w2(1))
+            z_g = [claim_product(b, hf) for hf in range(2)]
+            for hf in range(2):
+                zq[hf].append(quantise("zq%d%d" % (b, hf), z_g[hf], PC // 2))
+
+        def second_stage(c, w_codes, w_scales, x, width, bias):
+            acc = ps3.tile([P, width], F32, name="acc3")
+            for b in range(2):
+                nc.tensor.matmul_mx(
+                    out=acc[:],
+                    lhsT=w_codes[b][:, c * P : (c + 1) * P].bitcast(FP8X4),
+                    lhsT_scale=w_scales[b][:, c * P : (c + 1) * P],
+                    rhs=x[b][0][:].bitcast(FP8X4),
+                    rhs_scale=x[b][1][:],
+                    start=(b == 0),
+                    stop=(b == 1),
+                )
+            y = ring.tile([P, width], F32, name="y", bufs=6)
+            if bias is None:
+                nc.scalar.copy(y[:], acc[:])
+            else:
+                nc.scalar.activation(y[:], acc[:], ACT.Identity, bias=bias)
+            return y
+
+        for hf in range(2):
+            cols = slice(hf * PC // 2, (hf + 1) * PC // 2)
+            for c in range(3):
+                y = second_stage(c, [w4_w[:, b, :] for b in range(2)], [w4_s[:, b, :] for b in range(2)], zq[hf], PC // 2, None)
+                nc.vector.tensor_tensor(pages[c][:].indirect(l_offs4[:, 16 * hf : 16 * (hf + 1)]), y[:], wg2_t[:, cols], ALU.mult)
+
+        w3q = []
+        for b in range(2):
+            g = woven("w3_g%d" % b, N)
+            nc.scalar.copy(weave_out(g[:]), weave_in(w3_raw[b][:]))
+            w3q.append(quantise("w3q%d" % b, g, N))
+
+        for j0, width in ((0, 256), (256, 256), (512, 512)):
+            cols = slice(j0, j0 + width)
+            hq = []
+            for b in range(2):
+                g = woven("h_g%d_%d" % (j0, b), width)
+                for k0 in range(0, width, 256):
+                    nc.scalar.copy(weave_out(g[:, PACK * k0 : PACK * (k0 + 256)]), weave_in(h1[b][:, :, j0 + k0 : j0 + k0 + 256]))
+                hq.append(quantise("hq%d_%d" % (j0, b), g, width))
+            for c in range(3):
+                y = second_stage(c, [w[0][:] for w in w3q], [w[1][:] for w in w3q], hq, width, d_t[:, c : c + 1])
+                nc.vector.tensor_tensor(
+                    pages[c][:].indirect(l_offs3[:, j0 // 16 : (j0 + width) // 16]), y[:], wg1_t[:, cols], ALU.mult
+                )
+        for c in range(3):
+            nc.sync.dma_start(out[c * P : (c + 1) * P, :], pages[c][:])

@@ -46,22 +46,22 @@ def tile_list_repair_estimate_features_kernel(
             nc.sync.dma_start(t[:], src)
             return t
 
-        def zeroed(name, shape):
+        def zeroed(name, shape, engine):
             t = held(name, shape, U8)
-            nc.vector.memset(t[:].bitcast(I32), 0)
+            engine.memset(t[:].bitcast(I32), 0)
             return t
 
-        tab_s = zeroed("tab_s", [P, T])
-        w1_s = zeroed("w1_s", [P, 2, H])
-        tab2_s = zeroed("tab2_s", [P, T])
-        v_s1 = zeroed("v_s1", [P, S])
-        w4_s = zeroed("w4_s", [P, 2, N])
+        tab_s = zeroed("tab_s", [P, T], nc.vector)
+        w1_s = zeroed("w1_s", [P, 2, H], nc.gpsimd)
+        tab2_s = zeroed("tab2_s", [P, T], nc.vector)
+        v_s1 = zeroed("v_s1", [P, S], nc.vector)
+        w4_s = zeroed("w4_s", [P, 2, N], nc.vector)
 
         l_offs = load_list("l_offs", offs)
         for q in range(4):
-            nc.sync.dma_start(tab_s[32 * q : 32 * q + 8, :].bitcast(I32), tab_scales[:, 4 * q : 4 * q + 4, :].bitcast(I32))
+            nc.scalar.dma_start(tab_s[32 * q : 32 * q + 8, :].bitcast(I32), tab_scales[:, 4 * q : 4 * q + 4, :].bitcast(I32))
         for q in range(4):
-            nc.sync.dma_start(
+            nc.gpsimd.dma_start(
                 w1_s[32 * q : 32 * q + 4, :, :].bitcast(I32),
                 w1_scales[:, 4 * q : 4 * q + 4, :].rearrange("a r c -> r a c").bitcast(I32),
             )
@@ -74,10 +74,10 @@ def tile_list_repair_estimate_features_kernel(
             tab_w.append(t)
         w2_rows = w2.rearrange("(p j) c -> p j c", j=PACK)
         w2_raw = [held("w2_raw%d" % b, [P, PACK, KP], F32) for b in range(2)]
+        l_offs2 = load_list("l_offs2", offs2)
         nc.sync.dma_start(w2_raw[0][:], w2_rows[:, :, 0:KP])
         gain_t = held("gain_t", [P, 2, PACK], F32)
         nc.sync.dma_start(gain_t[:], gain.rearrange("(b p t) -> p b t", b=2, t=PACK))
-        l_offs2 = load_list("l_offs2", offs2)
         l_pos1 = load_list("l_pos1", pos1)
         for q in range(4):
             nc.sync.dma_start(tab2_s[32 * q : 32 * q + 4, :].bitcast(I32), tab2_scales[0, 4 * q : 4 * q + 4, :].bitcast(I32))
@@ -114,26 +114,22 @@ def tile_list_repair_estimate_features_kernel(
         v_s0 = held("v_s0", [P, S], U8)
         nc.vector.tensor_copy(v_s0[:], tab_s[:].indirect(l_offs[:]))
         for q in range(4):
-            nc.scalar.dma_start(v_s1[32 * q : 32 * q + 4, :].bitcast(I32), v_s0[32 * q + 4 : 32 * q + 8, :].bitcast(I32))
+            nc.gpsimd.dma_start(v_s1[32 * q : 32 * q + 4, :].bitcast(I32), v_s0[32 * q + 4 : 32 * q + 8, :].bitcast(I32))
         v_s = [v_s0, v_s1]
-        w1_sd = held("w1_sd", [P, 2, H], U8)
-        nc.vector.tensor_copy(
-            w1_sd[:].rearrange("p a (b t m) -> p (a b) t m", b=2, t=PACK),
-            w1_s[:].rearrange("p a (b m t) -> p (a b) t m", b=2, t=PACK),
-        )
         w1_wd = held("w1_wd", [P, 2, 2 * H], U8)
         nc.vector.tensor_copy(
             w1_wd[:].bitcast(U16).rearrange("p a (b t m) -> p (a b) t m", b=2, t=PACK),
             w1_w[:].bitcast(U16).rearrange("p a (b m t) -> p (a b) t m", b=2, t=PACK),
         )
-        v_w = []
+        w1_sd = held("w1_sd", [P, 2, H], U8)
+        nc.vector.tensor_copy(
+            w1_sd[:].rearrange("p a (b t m) -> p (a b) t m", b=2, t=PACK),
+            w1_s[:].rearrange("p a (b m t) -> p (a b) t m", b=2, t=PACK),
+        )
+        v_w = held("v_w", [P, 2, 2, COLS], U32, tag="tab_s")
         for hf in range(2):
-            row = []
             for a in range(2):
-                t = held("v_w%d%d" % (hf, a), [P, COLS], U32)
-                nc.vector.tensor_copy(t[:], tab_w[a][:].indirect(l_offs[:, 32 * hf : 32 * (hf + 1)]))
-                row.append(t)
-            v_w.append(row)
+                nc.vector.tensor_copy(v_w[:, hf, a, :], tab_w[a][:].indirect(l_offs[:, 32 * hf : 32 * (hf + 1)]))
         v2_s = held("v2_s", [P, PC], U8)
         nc.vector.tensor_copy(v2_s[:], tab2_s[:].indirect(l_offs2[:]))
         v2_w = held("v2_w", [P, PC], U32)
@@ -175,7 +171,7 @@ def tile_list_repair_estimate_features_kernel(
                         out=acc[:],
                         lhsT=w1_wd[:, a, 2 * c0 : 2 * (c0 + P)].bitcast(FP4X4),
                         lhsT_scale=w1_sd[:, a, c0 : c0 + P],
-                        rhs=v_w[hf][a][:].bitcast(FP8X4),
+                        rhs=v_w[:, hf, a, :].bitcast(FP8X4),
                         rhs_scale=v_s[a][:, cols],
                         start=(a == 0),
                         stop=(a == 1),
@@ -197,25 +193,26 @@ def tile_list_repair_estimate_features_kernel(
             nc.vector.tensor_copy(top[b][:, t, :], h1[b][:, t, :].indirect(l_pos1[:]))
             nc.vector.tensor_tensor(dif[b][:, t, :], acc[:], top[b][:, t, :], ALU.subtract)
 
-        def claim_product(b, hf):
-            g = woven("z_g%d%d" % (b, hf), PC // 2)
-            cols = slice(hf * PC // 2, (hf + 1) * PC // 2)
-            nc.vector.tensor_tensor(weave_out(g[:]), weave_in(dif[b][:, :, cols]), weave_in(top[b][:, :, cols]), ALU.mult)
+        def claim_product(b):
+            g = woven("z_g%d" % b, PC)
+            nc.vector.tensor_tensor(weave_out(g[:]), weave_in(dif[b][:]), weave_in(top[b][:]), ALU.mult)
             return g
 
-        zq = [[], []]
+        z_g = []
+        zq = []
         for b in range(2):
             for t in range(PACK):
                 line_features(b, t)
                 claim_difference(b, t)
                 if b == 0 and t == 1:
                     w2q.append(round_w2(1))
-            z_g = [claim_product(b, hf) for hf in range(2)]
-            for hf in range(2):
-                zq[hf].append(quantise("zq%d%d" % (b, hf), z_g[hf], PC // 2))
+                if b == 1 and t == 0:
+                    zq.append(quantise("zq0", z_g[0], PC))
+            z_g.append(claim_product(b))
+        zq.append(quantise("zq1", z_g[1], PC))
 
-        def second_stage(c, w_codes, w_scales, x, width, bias):
-            acc = ps3.tile([P, width], F32, name="acc3")
+        def second_stage(c, w_codes, w_scales, x, bias):
+            acc = ps3.tile([P, COLS], F32, name="acc3")
             for b in range(2):
                 nc.tensor.matmul_mx(
                     out=acc[:],
@@ -226,18 +223,16 @@ def tile_list_repair_estimate_features_kernel(
                     start=(b == 0),
                     stop=(b == 1),
                 )
-            y = ring.tile([P, width], F32, name="y", bufs=6)
+            y = ring.tile([P, COLS], F32, name="y", bufs=6)
             if bias is None:
                 nc.scalar.copy(y[:], acc[:])
             else:
                 nc.scalar.activation(y[:], acc[:], ACT.Identity, bias=bias)
             return y
 
-        for hf in range(2):
-            cols = slice(hf * PC // 2, (hf + 1) * PC // 2)
-            for c in range(3):
-                y = second_stage(c, [w4_w[:, b, :] for b in range(2)], [w4_s[:, b, :] for b in range(2)], zq[hf], PC // 2, None)
-                nc.vector.tensor_tensor(pages[c][:].indirect(l_offs4[:, 16 * hf : 16 * (hf + 1)]), y[:], wg2_t[:, cols], ALU.mult)
+        for c in range(3):
+            y = second_stage(c, [w4_w[:, b, :] for b in range(2)], [w4_s[:, b, :] for b in range(2)], zq, None)
+            nc.vector.tensor_tensor(pages[c][:].indirect(l_offs4[:]), y[:], wg2_t[:], ALU.mult)
 
         w3q = []
         for b in range(2):
@@ -245,18 +240,17 @@ def tile_list_repair_estimate_features_kernel(
             nc.scalar.copy(weave_out(g[:]), weave_in(w3_raw[b][:]))
             w3q.append(quantise("w3q%d" % b, g, N))
 
-        for j0, width in ((0, 256), (256, 256), (512, 512)):
-            cols = slice(j0, j0 + width)
+        for hf in range(2):
+            cols = slice(hf * COLS, (hf + 1) * COLS)
             hq = []
             for b in range(2):
-                g = woven("h_g%d_%d" % (j0, b), width)
-                for k0 in range(0, width, 256):
-                    nc.scalar.copy(weave_out(g[:, PACK * k0 : PACK * (k0 + 256)]), weave_in(h1[b][:, :, j0 + k0 : j0 + k0 + 256]))
-                hq.append(quantise("hq%d_%d" % (j0, b), g, width))
+                g = woven("h_g%d%d" % (hf, b), COLS)
+                nc.scalar.copy(weave_out(g[:]), weave_in(h1[b][:, :, cols]))
+                hq.append(quantise("hq%d%d" % (hf, b), g, COLS))
             for c in range(3):
-                y = second_stage(c, [w[0][:] for w in w3q], [w[1][:] for w in w3q], hq, width, d_t[:, c : c + 1])
+                y = second_stage(c, [w[0][:] for w in w3q], [w[1][:] for w in w3q], hq, d_t[:, c : c + 1])
                 nc.vector.tensor_tensor(
-                    pages[c][:].indirect(l_offs3[:, j0 // 16 : (j0 + width) // 16]), y[:], wg1_t[:, cols], ALU.mult
+                    pages[c][:].indirect(l_offs3[:, 32 * hf : 32 * (hf + 1)]), y[:], wg1_t[:, cols], ALU.mult
                 )
         for c in range(3):
             nc.sync.dma_start(out[c * P : (c + 1) * P, :], pages[c][:])

@@ -30,7 +30,7 @@ def tile_list_repair_estimate_features_kernel(
     with ExitStack() as ctx:
         keep = ctx.enter_context(tc.tile_pool(name="keep", bufs=1))
         ring = ctx.enter_context(tc.tile_pool(name="ring", bufs=3))
-        weave = ctx.enter_context(tc.tile_pool(name="weave", bufs=4))
+        weave = ctx.enter_context(tc.tile_pool(name="weave", bufs=3))
         ps1 = ctx.enter_context(tc.psum_pool(name="ps1", bufs=2))
         ps2 = ctx.enter_context(tc.psum_pool(name="ps2", bufs=2))
         ps3 = ctx.enter_context(tc.psum_pool(name="ps3", bufs=2))
@@ -52,16 +52,16 @@ def tile_list_repair_estimate_features_kernel(
             return t
 
         tab_s = zeroed("tab_s", [P, T], nc.vector)
-        w1_s = zeroed("w1_s", [P, 2, H], nc.gpsimd)
+        w1_s = zeroed("w1_s", [P, 2, H], nc.vector)
         tab2_s = zeroed("tab2_s", [P, T], nc.vector)
         v_s1 = zeroed("v_s1", [P, S], nc.vector)
         w4_s = zeroed("w4_s", [P, 2, N], nc.vector)
 
         l_offs = load_list("l_offs", offs)
         for q in range(4):
-            nc.scalar.dma_start(tab_s[32 * q : 32 * q + 8, :].bitcast(I32), tab_scales[:, 4 * q : 4 * q + 4, :].bitcast(I32))
+            nc.sync.dma_start(tab_s[32 * q : 32 * q + 8, :].bitcast(I32), tab_scales[:, 4 * q : 4 * q + 4, :].bitcast(I32))
         for q in range(4):
-            nc.gpsimd.dma_start(
+            nc.sync.dma_start(
                 w1_s[32 * q : 32 * q + 4, :, :].bitcast(I32),
                 w1_scales[:, 4 * q : 4 * q + 4, :].rearrange("a r c -> r a c").bitcast(I32),
             )
@@ -113,23 +113,26 @@ def tile_list_repair_estimate_features_kernel(
 
         v_s0 = held("v_s0", [P, S], U8)
         nc.vector.tensor_copy(v_s0[:], tab_s[:].indirect(l_offs[:]))
-        for q in range(4):
-            nc.gpsimd.dma_start(v_s1[32 * q : 32 * q + 4, :].bitcast(I32), v_s0[32 * q + 4 : 32 * q + 8, :].bitcast(I32))
+        nc.scalar.dma_start(v_s1[0:100, :].bitcast(I32), v_s0[4:104, :].bitcast(I32))
         v_s = [v_s0, v_s1]
-        w1_wd = held("w1_wd", [P, 2, 2 * H], U8)
-        nc.vector.tensor_copy(
-            w1_wd[:].bitcast(U16).rearrange("p a (b t m) -> p (a b) t m", b=2, t=PACK),
-            w1_w[:].bitcast(U16).rearrange("p a (b m t) -> p (a b) t m", b=2, t=PACK),
-        )
         w1_sd = held("w1_sd", [P, 2, H], U8)
         nc.vector.tensor_copy(
             w1_sd[:].rearrange("p a (b t m) -> p (a b) t m", b=2, t=PACK),
             w1_s[:].rearrange("p a (b m t) -> p (a b) t m", b=2, t=PACK),
         )
-        v_w = held("v_w", [P, 2, 2, COLS], U32, tag="tab_s")
+        w1_wd = held("w1_wd", [P, 2, 2 * H], U8)
+        nc.vector.tensor_copy(
+            w1_wd[:].bitcast(U16).rearrange("p a (b t m) -> p (a b) t m", b=2, t=PACK),
+            w1_w[:].bitcast(U16).rearrange("p a (b m t) -> p (a b) t m", b=2, t=PACK),
+        )
+        v_w = []
         for hf in range(2):
+            row = []
             for a in range(2):
-                nc.vector.tensor_copy(v_w[:, hf, a, :], tab_w[a][:].indirect(l_offs[:, 32 * hf : 32 * (hf + 1)]))
+                t = held("v_w%d%d" % (hf, a), [P, COLS], U32)
+                nc.vector.tensor_copy(t[:], tab_w[a][:].indirect(l_offs[:, 32 * hf : 32 * (hf + 1)]))
+                row.append(t)
+            v_w.append(row)
         v2_s = held("v2_s", [P, PC], U8)
         nc.vector.tensor_copy(v2_s[:], tab2_s[:].indirect(l_offs2[:]))
         v2_w = held("v2_w", [P, PC], U32)
@@ -143,7 +146,7 @@ def tile_list_repair_estimate_features_kernel(
 
         def round_w2(b):
             g = woven("w2_g%d" % b, KP)
-            nc.scalar.copy(
+            (nc.vector.tensor_copy if b == 0 else nc.scalar.copy)(
                 g[:].rearrange("p (t m j) -> p m j t", t=PACK, j=PACK),
                 w2_raw[b][:].rearrange("p j (m t) -> p m j t", t=PACK),
             )
@@ -171,7 +174,7 @@ def tile_list_repair_estimate_features_kernel(
                         out=acc[:],
                         lhsT=w1_wd[:, a, 2 * c0 : 2 * (c0 + P)].bitcast(FP4X4),
                         lhsT_scale=w1_sd[:, a, c0 : c0 + P],
-                        rhs=v_w[:, hf, a, :].bitcast(FP8X4),
+                        rhs=v_w[hf][a][:].bitcast(FP8X4),
                         rhs_scale=v_s[a][:, cols],
                         start=(a == 0),
                         stop=(a == 1),
@@ -211,7 +214,7 @@ def tile_list_repair_estimate_features_kernel(
             z_g.append(claim_product(b))
         zq.append(quantise("zq1", z_g[1], PC))
 
-        def second_stage(c, w_codes, w_scales, x, bias):
+        def second_stage(c, w_codes, w_scales, x, bias, tag=None):
             acc = ps3.tile([P, COLS], F32, name="acc3")
             for b in range(2):
                 nc.tensor.matmul_mx(
@@ -223,16 +226,15 @@ def tile_list_repair_estimate_features_kernel(
                     start=(b == 0),
                     stop=(b == 1),
                 )
-            y = ring.tile([P, COLS], F32, name="y", bufs=6)
+            if tag is None:
+                y = ring.tile([P, COLS], F32, name="y", bufs=6)
+            else:
+                y = held("y_" + tag, [P, COLS], F32, tag=tag)
             if bias is None:
                 nc.scalar.copy(y[:], acc[:])
             else:
                 nc.scalar.activation(y[:], acc[:], ACT.Identity, bias=bias)
             return y
-
-        for c in range(3):
-            y = second_stage(c, [w4_w[:, b, :] for b in range(2)], [w4_s[:, b, :] for b in range(2)], zq, None)
-            nc.vector.tensor_tensor(pages[c][:].indirect(l_offs4[:]), y[:], wg2_t[:], ALU.mult)
 
         w3q = []
         for b in range(2):
@@ -240,17 +242,40 @@ def tile_list_repair_estimate_features_kernel(
             nc.scalar.copy(weave_out(g[:]), weave_in(w3_raw[b][:]))
             w3q.append(quantise("w3q%d" % b, g, N))
 
-        for hf in range(2):
+        def quantise_lines(hf):
             cols = slice(hf * COLS, (hf + 1) * COLS)
             hq = []
             for b in range(2):
-                g = woven("h_g%d%d" % (hf, b), COLS)
+                if b == 0:
+                    g = held("h_g%d0" % hf, [P, PACK * COLS], BF16, tag="first%d" % hf)
+                else:
+                    g = woven("h_g%d1" % hf, COLS)
                 nc.scalar.copy(weave_out(g[:]), weave_in(h1[b][:, :, cols]))
                 hq.append(quantise("hq%d%d" % (hf, b), g, COLS))
-            for c in range(3):
-                y = second_stage(c, [w[0][:] for w in w3q], [w[1][:] for w in w3q], hq, d_t[:, c : c + 1])
-                nc.vector.tensor_tensor(
-                    pages[c][:].indirect(l_offs3[:, 32 * hf : 32 * (hf + 1)]), y[:], wg1_t[:, cols], ALU.mult
-                )
+            return hq
+
+        w4q = ([w4_w[:, b, :] for b in range(2)], [w4_s[:, b, :] for b in range(2)])
+        w3p = ([w[0][:] for w in w3q], [w[1][:] for w in w3q])
+
+        def put_claims(c, tag=None):
+            y = second_stage(c, w4q[0], w4q[1], zq, None, tag)
+            nc.vector.tensor_tensor(pages[c][:].indirect(l_offs4[:]), y[:], wg2_t[:], ALU.mult)
+
+        def put_lines(hf, hq, c, tag=None):
+            y = second_stage(c, w3p[0], w3p[1], hq, d_t[:, c : c + 1], tag)
+            nc.vector.tensor_tensor(
+                pages[c][:].indirect(l_offs3[:, 32 * hf : 32 * (hf + 1)]), y[:], wg1_t[:, hf * COLS : (hf + 1) * COLS], ALU.mult
+            )
+
+        put_claims(0)
+        put_claims(1)
+        hq0 = quantise_lines(0)
+        put_claims(2, "first0")
+        put_lines(0, hq0, 0)
+        put_lines(0, hq0, 1)
+        hq1 = quantise_lines(1)
+        put_lines(0, hq0, 2, "first1")
+        for c in range(3):
+            put_lines(1, hq1, c)
         for c in range(3):
             nc.sync.dma_start(out[c * P : (c + 1) * P, :], pages[c][:])

@@ -138,19 +138,21 @@ def tile_list_repair_estimate_features_kernel(
         v2_w = held("v2_w", [P, PC], U32)
         nc.vector.tensor_copy(v2_w[:], tab2_w[:].indirect(l_offs2[:]))
 
-        def quantise(name, src, width):
+        def quantise(name, src, width, tag=None):
             codes = held(name + "_w", [P, width], U32)
-            scales = held(name + "_s", [P, width], U8)
-            nc.vector.quantize_mx(out=codes[:].bitcast(FP8X4), scales=scales[:], in_=src[:])
+            scales = held(name + "_s", [P, width], U8, tag=tag)
+            nc.vector.quantize_mx(out=codes[:].bitcast(FP8X4), scales=scales[:], in_=src)
             return codes, scales
 
         def round_w2(b):
-            g = woven("w2_g%d" % b, KP)
-            (nc.vector.tensor_copy if b == 0 else nc.scalar.copy)(
-                g[:].rearrange("p (t m j) -> p m j t", t=PACK, j=PACK),
-                w2_raw[b][:].rearrange("p j (m t) -> p m j t", t=PACK),
-            )
-            return quantise("w2q%d" % b, g, KP)
+            g = held("w2_g%d" % b, [P, PACK * KP], BF16, tag="w2_g")
+            dst = g[:].rearrange("p (t m j) -> p m j t", t=PACK, j=PACK)
+            src = w2_raw[b][:].rearrange("p j (m t) -> p m j t", t=PACK)
+            if b == 0:
+                nc.vector.tensor_copy(dst, src)
+            else:
+                nc.gpsimd.tensor_scalar(dst.rearrange("p m j t -> p t m j"), src.rearrange("p m j t -> p t m j"), 1.0, 0.0, ALU.mult, ALU.add)
+            return quantise("w2q%d" % b, g[:], KP)
 
         def weave_out(ap):
             return ap.rearrange("p (c i t) -> p c t i", i=4, t=PACK)
@@ -164,7 +166,10 @@ def tile_list_repair_estimate_features_kernel(
         w2q = [round_w2(0)]
 
         def line_features(b, t):
-            th = ring.tile([P, S], F32, name="th")
+            if (b, t) == (1, PACK - 1):
+                th = held("th_last", [P, S], F32, tag="late")
+            else:
+                th = ring.tile([P, S], F32, name="th")
             c0 = b * KP + t * P
             for hf in range(2):
                 cols = slice(hf * COLS, (hf + 1) * COLS)
@@ -198,7 +203,15 @@ def tile_list_repair_estimate_features_kernel(
 
         def claim_product(b):
             g = woven("z_g%d" % b, PC)
-            nc.vector.tensor_tensor(weave_out(g[:]), weave_in(dif[b][:]), weave_in(top[b][:]), ALU.mult)
+            if b == 0:
+                nc.gpsimd.tensor_tensor(
+                    g[:].rearrange("p (j t) -> p j t", t=PACK),
+                    dif[b][:].rearrange("p t j -> p j t"),
+                    top[b][:].rearrange("p t j -> p j t"),
+                    ALU.mult,
+                )
+            else:
+                nc.vector.tensor_tensor(weave_out(g[:]), weave_in(dif[b][:]), weave_in(top[b][:]), ALU.mult)
             return g
 
         z_g = []
@@ -209,10 +222,10 @@ def tile_list_repair_estimate_features_kernel(
                 claim_difference(b, t)
                 if b == 0 and t == 1:
                     w2q.append(round_w2(1))
-                if b == 1 and t == 0:
-                    zq.append(quantise("zq0", z_g[0], PC))
+                if b == 1 and t == 3:
+                    zq.append(quantise("zq0", z_g[0][:], PC, tag="gain_t"))
             z_g.append(claim_product(b))
-        zq.append(quantise("zq1", z_g[1], PC))
+        zq.append(quantise("zq1", z_g[1][:], PC))
 
         def second_stage(c, w_codes, w_scales, x, bias, tag=None):
             acc = ps3.tile([P, COLS], F32, name="acc3")
@@ -237,21 +250,21 @@ def tile_list_repair_estimate_features_kernel(
             return y
 
         w3q = []
+        w3_g = held("w3_g", [P, 2, PACK * N], BF16, tag="late")
         for b in range(2):
-            g = woven("w3_g%d" % b, N)
-            nc.scalar.copy(weave_out(g[:]), weave_in(w3_raw[b][:]))
-            w3q.append(quantise("w3q%d" % b, g, N))
+            nc.scalar.copy(weave_out(w3_g[:, b, :]), weave_in(w3_raw[b][:]))
+            w3q.append(quantise("w3q%d" % b, w3_g[:, b, :], N))
 
         def quantise_lines(hf):
             cols = slice(hf * COLS, (hf + 1) * COLS)
             hq = []
             for b in range(2):
-                if b == 0:
-                    g = held("h_g%d0" % hf, [P, PACK * COLS], BF16, tag="first%d" % hf)
+                if (hf, b) == (1, 1):
+                    g = woven("h_g11", COLS)
                 else:
-                    g = woven("h_g%d1" % hf, COLS)
+                    g = held("h_g%d%d" % (hf, b), [P, PACK * COLS], BF16, tag="late" if (hf, b) == (0, 0) else "later")
                 nc.scalar.copy(weave_out(g[:]), weave_in(h1[b][:, :, cols]))
-                hq.append(quantise("hq%d%d" % (hf, b), g, COLS))
+                hq.append(quantise("hq%d%d" % (hf, b), g[:], COLS))
             return hq
 
         w4q = ([w4_w[:, b, :] for b in range(2)], [w4_s[:, b, :] for b in range(2)])
@@ -270,12 +283,14 @@ def tile_list_repair_estimate_features_kernel(
         put_claims(0)
         put_claims(1)
         hq0 = quantise_lines(0)
-        put_claims(2, "first0")
+        put_claims(2, "late")
         put_lines(0, hq0, 0)
         put_lines(0, hq0, 1)
         hq1 = quantise_lines(1)
-        put_lines(0, hq0, 2, "first1")
+        put_lines(0, hq0, 2, "later")
         for c in range(3):
             put_lines(1, hq1, c)
         for c in range(3):
-            nc.sync.dma_start(out[c * P : (c + 1) * P, :], pages[c][:])
+            for hf in range(2):
+                cols = slice(hf * T2 // 2, (hf + 1) * T2 // 2)
+                nc.sync.dma_start(out[c * P : (c + 1) * P, cols], pages[c][:, cols])

@@ -20,6 +20,10 @@ P = 128
 PACK = 4
 KP = P * PACK
 COLS = 512
+QUADS = 4
+LIST_COLS = COLS // 16
+PAGES = N // P
+PLANE_ROWS = 32 * (QUADS - 1) + 4
 
 
 def tile_list_repair_estimate_features_kernel(
@@ -42,25 +46,25 @@ def tile_list_repair_estimate_features_kernel(
             return weave.tile([P, PACK * width], BF16, name=name, tag="woven", align_bytes=64)
 
         def load_list(name, src):
-            t = keep.tile(list(src.shape), U16, name=name)
-            nc.sync.dma_start(t[:], src)
-            return t
+            tile = keep.tile(list(src.shape), U16, name=name)
+            nc.sync.dma_start(tile[:], src)
+            return tile
 
-        def zeroed(name, shape, engine):
-            t = held(name, shape, U8)
-            engine.memset(t[:].bitcast(I32), 0)
-            return t
+        def zeroed(name, shape):
+            tile = held(name, shape, U8)
+            nc.vector.memset(tile[:].bitcast(I32), 0)
+            return tile
 
-        tab_s = zeroed("tab_s", [P, T], nc.vector)
-        w1_s = zeroed("w1_s", [P, 2, H], nc.vector)
-        tab2_s = zeroed("tab2_s", [P, T], nc.vector)
-        v_s1 = zeroed("v_s1", [P, S], nc.vector)
-        w4_s = zeroed("w4_s", [P, 2, N], nc.vector)
+        tab_s = zeroed("tab_s", [P, T])
+        w1_s = zeroed("w1_s", [P, 2, H])
+        tab2_s = zeroed("tab2_s", [P, T])
+        v_s1 = zeroed("v_s1", [P, S])
+        w4_s = zeroed("w4_s", [P, 2, N])
 
         l_offs = load_list("l_offs", offs)
-        for q in range(4):
+        for q in range(QUADS):
             nc.sync.dma_start(tab_s[32 * q : 32 * q + 8, :].bitcast(I32), tab_scales[:, 4 * q : 4 * q + 4, :].bitcast(I32))
-        for q in range(4):
+        for q in range(QUADS):
             nc.sync.dma_start(
                 w1_s[32 * q : 32 * q + 4, :, :].bitcast(I32),
                 w1_scales[:, 4 * q : 4 * q + 4, :].rearrange("a r c -> r a c").bitcast(I32),
@@ -69,9 +73,9 @@ def tile_list_repair_estimate_features_kernel(
         nc.sync.dma_start(w1_w[:].bitcast(I32), w1_words.rearrange("a p c -> p a c").bitcast(I32))
         tab_w = []
         for a in range(2):
-            t = held("tab_w%d" % a, [P, T], U32)
-            nc.sync.dma_start(t[:].bitcast(I32), tab_words[a].rearrange("p t i -> p (t i)").bitcast(I32))
-            tab_w.append(t)
+            tile = held("tab_w%d" % a, [P, T], U32)
+            nc.sync.dma_start(tile[:].bitcast(I32), tab_words[a].rearrange("p t i -> p (t i)").bitcast(I32))
+            tab_w.append(tile)
         w2_rows = w2.rearrange("(p j) c -> p j c", j=PACK)
         w2_raw = [held("w2_raw%d" % b, [P, PACK, KP], F32) for b in range(2)]
         l_offs2 = load_list("l_offs2", offs2)
@@ -79,41 +83,41 @@ def tile_list_repair_estimate_features_kernel(
         gain_t = held("gain_t", [P, 2, PACK], F32)
         nc.sync.dma_start(gain_t[:], gain.rearrange("(b p t) -> p b t", b=2, t=PACK))
         l_pos1 = load_list("l_pos1", pos1)
-        for q in range(4):
+        for q in range(QUADS):
             nc.sync.dma_start(tab2_s[32 * q : 32 * q + 4, :].bitcast(I32), tab2_scales[0, 4 * q : 4 * q + 4, :].bitcast(I32))
         tab2_w = held("tab2_w", [P, T], U32)
         nc.sync.dma_start(tab2_w[:].bitcast(I32), tab2_words[0].rearrange("p t i -> p (t i)").bitcast(I32))
         nc.sync.dma_start(w2_raw[1][:], w2_rows[:, :, KP : 2 * KP])
         w4_w = held("w4_w", [P, 2, N], U32)
         nc.sync.dma_start(w4_w[:].bitcast(I32), w4_words.rearrange("a p c i -> p a (c i)").bitcast(I32))
-        for q in range(4):
+        for q in range(QUADS):
             nc.sync.dma_start(
                 w4_s[32 * q : 32 * q + 4, :, :].bitcast(I32),
                 w4_scales[:, 4 * q : 4 * q + 4, :].rearrange("a r c -> r a c").bitcast(I32),
             )
         w3_raw = []
         for b in range(2):
-            t = held("w3_raw%d" % b, [P, PACK, N], F32)
-            nc.sync.dma_start(t[:], w3[b * KP : (b + 1) * KP, :].rearrange("(p j) n -> p j n", j=PACK))
-            w3_raw.append(t)
+            tile = held("w3_raw%d" % b, [P, PACK, N], F32)
+            nc.sync.dma_start(tile[:], w3[b * KP : (b + 1) * KP, :].rearrange("(p j) n -> p j n", j=PACK))
+            w3_raw.append(tile)
         l_offs4 = load_list("l_offs4", offs4)
         l_offs3 = load_list("l_offs3", offs3)
         wg2_t = held("wg2_t", [P, PC], F32)
         nc.sync.dma_start(wg2_t[:], wg2)
         pages = []
-        for c in range(3):
-            t = held("page%d" % c, [P, T2], F32)
-            nc.sync.dma_start(t[:], page1[c * P : (c + 1) * P, :])
-            pages.append(t)
+        for c in range(PAGES):
+            tile = held("page%d" % c, [P, T2], F32)
+            nc.sync.dma_start(tile[:], page1[c * P : (c + 1) * P, :])
+            pages.append(tile)
         wg1_t = held("wg1_t", [P, S], F32)
         nc.sync.dma_start(wg1_t[:], wg1)
-        d_t = held("d_t", [P, 3], F32)
+        d_t = held("d_t", [P, PAGES], F32)
         with nc.allow_non_contiguous_dma(reason="one bias value for each partition"):
             nc.sync.dma_start(d_t[:], d.rearrange("(c p) -> p c", p=P))
 
         v_s0 = held("v_s0", [P, S], U8)
         nc.vector.tensor_copy(v_s0[:], tab_s[:].indirect(l_offs[:]))
-        nc.scalar.dma_start(v_s1[0:100, :].bitcast(I32), v_s0[4:104, :].bitcast(I32))
+        nc.scalar.dma_start(v_s1[0:PLANE_ROWS, :].bitcast(I32), v_s0[4 : PLANE_ROWS + 4, :].bitcast(I32))
         v_s = [v_s0, v_s1]
         w1_sd = held("w1_sd", [P, 2, H], U8)
         nc.vector.tensor_copy(
@@ -129,9 +133,9 @@ def tile_list_repair_estimate_features_kernel(
         for hf in range(2):
             row = []
             for a in range(2):
-                t = held("v_w%d%d" % (hf, a), [P, COLS], U32)
-                nc.vector.tensor_copy(t[:], tab_w[a][:].indirect(l_offs[:, 32 * hf : 32 * (hf + 1)]))
-                row.append(t)
+                tile = held("v_w%d%d" % (hf, a), [P, COLS], U32)
+                nc.vector.tensor_copy(tile[:], tab_w[a][:].indirect(l_offs[:, LIST_COLS * hf : LIST_COLS * (hf + 1)]))
+                row.append(tile)
             v_w.append(row)
         v2_s = held("v2_s", [P, PC], U8)
         nc.vector.tensor_copy(v2_s[:], tab2_s[:].indirect(l_offs2[:]))
@@ -144,14 +148,15 @@ def tile_list_repair_estimate_features_kernel(
             nc.vector.quantize_mx(out=codes[:].bitcast(FP8X4), scales=scales[:], in_=src)
             return codes, scales
 
-        def round_w2(b):
+        def quantise_w2(b):
             g = held("w2_g%d" % b, [P, PACK * KP], BF16, tag="w2_g")
             dst = g[:].rearrange("p (t m j) -> p m j t", t=PACK, j=PACK)
             src = w2_raw[b][:].rearrange("p j (m t) -> p m j t", t=PACK)
             if b == 0:
                 nc.vector.tensor_copy(dst, src)
             else:
-                nc.gpsimd.tensor_scalar(dst.rearrange("p m j t -> p t m j"), src.rearrange("p m j t -> p t m j"), 1.0, 0.0, ALU.mult, ALU.add)
+                nc.scalar.copy(dst[:, 0 : P // 2], src[:, 0 : P // 2])
+                nc.vector.tensor_copy(dst[:, P // 2 : P], src[:, P // 2 : P])
             return quantise("w2q%d" % b, g[:], KP)
 
         def weave_out(ap):
@@ -163,7 +168,7 @@ def tile_list_repair_estimate_features_kernel(
         h1 = [held("h1_%d" % b, [P, PACK, S], F32) for b in range(2)]
         top = [held("top%d" % b, [P, PACK, PC], F32) for b in range(2)]
         dif = [held("dif%d" % b, [P, PACK, PC], F32, tag="tab_w%d" % b) for b in range(2)]
-        w2q = [round_w2(0)]
+        w2q = [quantise_w2(0)]
 
         def line_features(b, t):
             if (b, t) == (1, PACK - 1):
@@ -203,15 +208,7 @@ def tile_list_repair_estimate_features_kernel(
 
         def claim_product(b):
             g = woven("z_g%d" % b, PC)
-            if b == 0:
-                nc.gpsimd.tensor_tensor(
-                    g[:].rearrange("p (j t) -> p j t", t=PACK),
-                    dif[b][:].rearrange("p t j -> p j t"),
-                    top[b][:].rearrange("p t j -> p j t"),
-                    ALU.mult,
-                )
-            else:
-                nc.vector.tensor_tensor(weave_out(g[:]), weave_in(dif[b][:]), weave_in(top[b][:]), ALU.mult)
+            nc.vector.tensor_tensor(weave_out(g[:]), weave_in(dif[b][:]), weave_in(top[b][:]), ALU.mult)
             return g
 
         z_g = []
@@ -220,14 +217,14 @@ def tile_list_repair_estimate_features_kernel(
             for t in range(PACK):
                 line_features(b, t)
                 claim_difference(b, t)
-                if b == 0 and t == 1:
-                    w2q.append(round_w2(1))
-                if b == 1 and t == 3:
+                if (b, t) == (0, 1):
+                    w2q.append(quantise_w2(1))
+                if (b, t) == (1, PACK - 1):
                     zq.append(quantise("zq0", z_g[0][:], PC, tag="gain_t"))
             z_g.append(claim_product(b))
         zq.append(quantise("zq1", z_g[1][:], PC))
 
-        def second_stage(c, w_codes, w_scales, x, bias, tag=None):
+        def second_stage(c, w_codes, w_scales, x, bias, tag):
             acc = ps3.tile([P, COLS], F32, name="acc3")
             for b in range(2):
                 nc.tensor.matmul_mx(
@@ -240,7 +237,7 @@ def tile_list_repair_estimate_features_kernel(
                     stop=(b == 1),
                 )
             if tag is None:
-                y = ring.tile([P, COLS], F32, name="y", bufs=6)
+                y = ring.tile([P, COLS], F32, name="y", bufs=2 * PAGES)
             else:
                 y = held("y_" + tag, [P, COLS], F32, tag=tag)
             if bias is None:
@@ -267,17 +264,22 @@ def tile_list_repair_estimate_features_kernel(
                 hq.append(quantise("hq%d%d" % (hf, b), g[:], COLS))
             return hq
 
-        w4q = ([w4_w[:, b, :] for b in range(2)], [w4_s[:, b, :] for b in range(2)])
-        w3p = ([w[0][:] for w in w3q], [w[1][:] for w in w3q])
+        w4_codes = [w4_w[:, b, :] for b in range(2)]
+        w4_planes = [w4_s[:, b, :] for b in range(2)]
+        w3_codes = [w[0][:] for w in w3q]
+        w3_planes = [w[1][:] for w in w3q]
 
         def put_claims(c, tag=None):
-            y = second_stage(c, w4q[0], w4q[1], zq, None, tag)
+            y = second_stage(c, w4_codes, w4_planes, zq, None, tag)
             nc.vector.tensor_tensor(pages[c][:].indirect(l_offs4[:]), y[:], wg2_t[:], ALU.mult)
 
         def put_lines(hf, hq, c, tag=None):
-            y = second_stage(c, w3p[0], w3p[1], hq, d_t[:, c : c + 1], tag)
+            y = second_stage(c, w3_codes, w3_planes, hq, d_t[:, c : c + 1], tag)
             nc.vector.tensor_tensor(
-                pages[c][:].indirect(l_offs3[:, 32 * hf : 32 * (hf + 1)]), y[:], wg1_t[:, hf * COLS : (hf + 1) * COLS], ALU.mult
+                pages[c][:].indirect(l_offs3[:, LIST_COLS * hf : LIST_COLS * (hf + 1)]),
+                y[:],
+                wg1_t[:, hf * COLS : (hf + 1) * COLS],
+                ALU.mult,
             )
 
         put_claims(0)
@@ -288,9 +290,9 @@ def tile_list_repair_estimate_features_kernel(
         put_lines(0, hq0, 1)
         hq1 = quantise_lines(1)
         put_lines(0, hq0, 2, "later")
-        for c in range(3):
+        for c in range(PAGES):
             put_lines(1, hq1, c)
-        for c in range(3):
-            for hf in range(2):
-                cols = slice(hf * T2 // 2, (hf + 1) * T2 // 2)
+        for c in range(PAGES):
+            for side in range(2):
+                cols = slice(side * T2 // 2, (side + 1) * T2 // 2)
                 nc.sync.dma_start(out[c * P : (c + 1) * P, cols], pages[c][:, cols])

from contextlib import ExitStack

import concourse.mybir as mybir

K, KB, H, N, T, S, PC, T2 = 1024, 512, 1024, 384, 2048, 1024, 512, 2048
FLOPS = 2 * (K * H * S + KB * H * PC + H * N * S + H * N * PC)

F32 = mybir.dt.float32
BF16 = mybir.dt.bfloat16
I32 = mybir.dt.int32
U32 = mybir.dt.uint32
U16 = mybir.dt.uint16
U8 = mybir.dt.uint8
FP8X4 = mybir.dt.float8_e4m3fn_x4
FP4X4 = mybir.dt.float4_e2m1fn_x4
ACT = mybir.ActivationFunctionType
ALU = mybir.AluOpType

P = 128
PACK = 4
KP = P * PACK
COLS = 512
QUADS = 4
LIST_COLS = COLS // 16
PAGES = N // P
PLANE_ROWS = 32 * (QUADS - 1) + 4


def tile_list_repair_estimate_features_kernel(
    tc, tab_words, tab_scales, tab2_words, tab2_scales, w1_words, w1_scales, gain, w2, w3, d,
    w4_words, w4_scales, page1, wg1, wg2, offs, offs2, pos1, offs3, offs4, out,
):
    nc = tc.nc
    with ExitStack() as ctx:
        keep = ctx.enter_context(tc.tile_pool(name="keep", bufs=1))
        ring = ctx.enter_context(tc.tile_pool(name="ring", bufs=3))
        weave = ctx.enter_context(tc.tile_pool(name="weave", bufs=3))
        ps1 = ctx.enter_context(tc.psum_pool(name="ps1", bufs=2))
        ps2 = ctx.enter_context(tc.psum_pool(name="ps2", bufs=2))
        ps3 = ctx.enter_context(tc.psum_pool(name="ps3", bufs=2))

        def held(name, shape, dtype, tag=None):
            return keep.tile(shape, dtype, name=name, tag=tag or name, align_bytes=64)

        def woven(name, width):
            return weave.tile([P, PACK * width], BF16, name=name, tag="woven", align_bytes=64)

        def load_list(name, src):
            tile = keep.tile(list(src.shape), U16, name=name)
            nc.sync.dma_start(tile[:], src)
            return tile

        def zeroed(name, shape):
            tile = held(name, shape, U8)
            nc.vector.memset(tile[:].bitcast(I32), 0)
            return tile

        tab_s = zeroed("tab_s", [P, T])
        w1_s = zeroed("w1_s", [P, 2, H])
        tab2_s = zeroed("tab2_s", [P, T])
        v_s1 = zeroed("v_s1", [P, S])
        w4_s = zeroed("w4_s", [P, 2, N])

        l_offs = load_list("l_offs", offs)
        for q in range(QUADS):
            nc.sync.dma_start(tab_s[32 * q : 32 * q + 8, :].bitcast(I32), tab_scales[:, 4 * q : 4 * q + 4, :].bitcast(I32))
        for q in range(QUADS):
            nc.sync.dma_start(
                w1_s[32 * q : 32 * q + 4, :, :].bitcast(I32),
                w1_scales[:, 4 * q : 4 * q + 4, :].rearrange("a r c -> r a c").bitcast(I32),
            )
        w1_w = held("w1_w", [P, 2, 2 * H], U8)
        nc.sync.dma_start(w1_w[:].bitcast(I32), w1_words.rearrange("a p c -> p a c").bitcast(I32))
        tab_w = []
        for a in range(2):
            tile = held("tab_w%d" % a, [P, T], U32)
            nc.sync.dma_start(tile[:].bitcast(I32), tab_words[a].rearrange("p t i -> p (t i)").bitcast(I32))
            tab_w.append(tile)
        w2_rows = w2.rearrange("(p j) c -> p j c", j=PACK)
        w2_raw = [held("w2_raw%d" % b, [P, PACK, KP], F32) for b in range(2)]
        l_offs2 = load_list("l_offs2", offs2)
        nc.sync.dma_start(w2_raw[0][:], w2_rows[:, :, 0:KP])
        gain_t = held("gain_t", [P, 2, PACK], F32)
        nc.sync.dma_start(gain_t[:], gain.rearrange("(b p t) -> p b t", b=2, t=PACK))
        l_pos1 = load_list("l_pos1", pos1)
        for q in range(QUADS):
            nc.sync.dma_start(tab2_s[32 * q : 32 * q + 4, :].bitcast(I32), tab2_scales[0, 4 * q : 4 * q + 4, :].bitcast(I32))
        tab2_w = held("tab2_w", [P, T], U32)
        nc.sync.dma_start(tab2_w[:].bitcast(I32), tab2_words[0].rearrange("p t i -> p (t i)").bitcast(I32))
        nc.sync.dma_start(w2_raw[1][:], w2_rows[:, :, KP : 2 * KP])
        w4_w = held("w4_w", [P, 2, N], U32)
        nc.sync.dma_start(w4_w[:].bitcast(I32), w4_words.rearrange("a p c i -> p a (c i)").bitcast(I32))
        for q in range(QUADS):
            nc.sync.dma_start(
                w4_s[32 * q : 32 * q + 4, :, :].bitcast(I32),
                w4_scales[:, 4 * q : 4 * q + 4, :].rearrange("a r c -> r a c").bitcast(I32),
            )
        w3_raw = []
        for b in range(2):
            tile = held("w3_raw%d" % b, [P, PACK, N], F32)
            nc.sync.dma_start(tile[:], w3[b * KP : (b + 1) * KP, :].rearrange("(p j) n -> p j n", j=PACK))
            w3_raw.append(tile)
        l_offs4 = load_list("l_offs4", offs4)
        l_offs3 = load_list("l_offs3", offs3)
        wg2_t = held("wg2_t", [P, PC], F32)
        nc.sync.dma_start(wg2_t[:], wg2)
        pages = []
        for c in range(PAGES):
            tile = held("page%d" % c, [P, T2], F32)
            nc.sync.dma_start(tile[:], page1[c * P : (c + 1) * P, :])
            pages.append(tile)
        wg1_t = held("wg1_t", [P, S], F32)
        nc.sync.dma_start(wg1_t[:], wg1)
        d_t = held("d_t", [P, PAGES], F32)
        with nc.allow_non_contiguous_dma(reason="one bias value for each partition"):
            nc.sync.dma_start(d_t[:], d.rearrange("(c p) -> p c", p=P))

        v_s0 = held("v_s0", [P, S], U8)
        nc.vector.tensor_copy(v_s0[:], tab_s[:].indirect(l_offs[:]))
        nc.scalar.dma_start(v_s1[0:PLANE_ROWS, :].bitcast(I32), v_s0[4 : PLANE_ROWS + 4, :].bitcast(I32))
        v_s = [v_s0, v_s1]
        w1_sd = held("w1_sd", [P, 2, H], U8)
        nc.vector.tensor_copy(
            w1_sd[:].rearrange("p a (b t m) -> p (a b) t m", b=2, t=PACK),
            w1_s[:].rearrange("p a (b m t) -> p (a b) t m", b=2, t=PACK),
        )
        w1_wd = held("w1_wd", [P, 2, 2 * H], U8)
        nc.vector.tensor_copy(
            w1_wd[:].bitcast(U16).rearrange("p a (b t m) -> p (a b) t m", b=2, t=PACK),
            w1_w[:].bitcast(U16).rearrange("p a (b m t) -> p (a b) t m", b=2, t=PACK),
        )
        v_w = []
        for hf in range(2):
            row = []
            for a in range(2):
                tile = held("v_w%d%d" % (hf, a), [P, COLS], U32)
                nc.vector.tensor_copy(tile[:], tab_w[a][:].indirect(l_offs[:, LIST_COLS * hf : LIST_COLS * (hf + 1)]))
                row.append(tile)
            v_w.append(row)
        v2_s = held("v2_s", [P, PC], U8)
        nc.vector.tensor_copy(v2_s[:], tab2_s[:].indirect(l_offs2[:]))
        v2_w = held("v2_w", [P, PC], U32)
        nc.vector.tensor_copy(v2_w[:], tab2_w[:].indirect(l_offs2[:]))

        def quantise(name, src, width, tag=None):
            codes = held(name + "_w", [P, width], U32)
            scales = held(name + "_s", [P, width], U8, tag=tag)
            nc.vector.quantize_mx(out=codes[:].bitcast(FP8X4), scales=scales[:], in_=src)
            return codes, scales

        def quantise_w2(b):
            g = held("w2_g%d" % b, [P, PACK * KP], BF16, tag="w2_g")
            dst = g[:].rearrange("p (t m j) -> p m j t", t=PACK, j=PACK)
            src = w2_raw[b][:].rearrange("p j (m t) -> p m j t", t=PACK)
            if b == 0:
                nc.vector.tensor_copy(dst, src)
            else:
                nc.scalar.copy(dst[:, 0 : P // 2], src[:, 0 : P // 2])
                nc.vector.tensor_copy(dst[:, P // 2 : P], src[:, P // 2 : P])
            return quantise("w2q%d" % b, g[:], KP)

        def weave_out(ap):
            return ap.rearrange("p (c i t) -> p c t i", i=4, t=PACK)

        def weave_in(ap):
            return ap.rearrange("p t (c i) -> p c t i", i=4)

        h1 = [held("h1_%d" % b, [P, PACK, S], F32) for b in range(2)]
        top = [held("top%d" % b, [P, PACK, PC], F32) for b in range(2)]
        dif = [held("dif%d" % b, [P, PACK, PC], F32, tag="tab_w%d" % b) for b in range(2)]
        w2q = [quantise_w2(0)]

        def line_features(b, t):
            if (b, t) == (1, PACK - 1):
                th = held("th_last", [P, S], F32, tag="late")
            else:
                th = ring.tile([P, S], F32, name="th")
            c0 = b * KP + t * P
            for hf in range(2):
                cols = slice(hf * COLS, (hf + 1) * COLS)
                acc = ps1.tile([P, COLS], F32, name="acc1_%d" % hf)
                for a in range(2):
                    nc.tensor.matmul_mx(
                        out=acc[:],
                        lhsT=w1_wd[:, a, 2 * c0 : 2 * (c0 + P)].bitcast(FP4X4),
                        lhsT_scale=w1_sd[:, a, c0 : c0 + P],
                        rhs=v_w[hf][a][:].bitcast(FP8X4),
                        rhs_scale=v_s[a][:, cols],
                        start=(a == 0),
                        stop=(a == 1),
                    )
                nc.scalar.activation(th[:, cols], acc[:], ACT.Tanh)
            nc.scalar.activation(h1[b][:, t, :], th[:], ACT.Copy, scale=gain_t[:, b, t : t + 1])

        def claim_difference(b, t):
            acc = ps2.tile([P, PC], F32, name="acc2")
            nc.tensor.matmul_mx(
                out=acc[:],
                lhsT=w2q[b][0][:, t * P : (t + 1) * P].bitcast(FP8X4),
                lhsT_scale=w2q[b][1][:, t * P : (t + 1) * P],
                rhs=v2_w[:].bitcast(FP8X4),
                rhs_scale=v2_s[:],
                start=True,
                stop=True,
            )
            nc.vector.tensor_copy(top[b][:, t, :], h1[b][:, t, :].indirect(l_pos1[:]))
            nc.vector.tensor_tensor(dif[b][:, t, :], acc[:], top[b][:, t, :], ALU.subtract)

        def claim_product(b):
            g = woven("z_g%d" % b, PC)
            nc.vector.tensor_tensor(weave_out(g[:]), weave_in(dif[b][:]), weave_in(top[b][:]), ALU.mult)
            return g

        z_g = []
        zq = []
        for b in range(2):
            for t in range(PACK):
                line_features(b, t)
                claim_difference(b, t)
                if (b, t) == (0, 1):
                    w2q.append(quantise_w2(1))
                if (b, t) == (1, PACK - 1):
                    zq.append(quantise("zq0", z_g[0][:], PC, tag="gain_t"))
            z_g.append(claim_product(b))
        zq.append(quantise("zq1", z_g[1][:], PC))

        def second_stage(c, w_codes, w_scales, x, bias, tag):
            acc = ps3.tile([P, COLS], F32, name="acc3")
            for b in range(2):
                nc.tensor.matmul_mx(
                    out=acc[:],
                    lhsT=w_codes[b][:, c * P : (c + 1) * P].bitcast(FP8X4),
                    lhsT_scale=w_scales[b][:, c * P : (c + 1) * P],
                    rhs=x[b][0][:].bitcast(FP8X4),
                    rhs_scale=x[b][1][:],
                    start=(b == 0),
                    stop=(b == 1),
                )
            if tag is None:
                y = ring.tile([P, COLS], F32, name="y", bufs=2 * PAGES)
            else:
                y = held("y_" + tag, [P, COLS], F32, tag=tag)
            if bias is None:
                nc.scalar.copy(y[:], acc[:])
            else:
                nc.scalar.activation(y[:], acc[:], ACT.Identity, bias=bias)
            return y

        w3q = []
        w3_g = held("w3_g", [P, 2, PACK * N], BF16, tag="late")
        for b in range(2):
            nc.scalar.copy(weave_out(w3_g[:, b, :]), weave_in(w3_raw[b][:]))
            w3q.append(quantise("w3q%d" % b, w3_g[:, b, :], N))

        def quantise_lines(hf):
            cols = slice(hf * COLS, (hf + 1) * COLS)
            hq = []
            for b in range(2):
                if (hf, b) == (1, 1):
                    g = woven("h_g11", COLS)
                else:
                    g = held("h_g%d%d" % (hf, b), [P, PACK * COLS], BF16, tag="late" if (hf, b) == (0, 0) else "later")
                nc.scalar.copy(weave_out(g[:]), weave_in(h1[b][:, :, cols]))
                hq.append(quantise("hq%d%d" % (hf, b), g[:], COLS))
            return hq

        w4_codes = [w4_w[:, b, :] for b in range(2)]
        w4_planes = [w4_s[:, b, :] for b in range(2)]
        w3_codes = [w[0][:] for w in w3q]
        w3_planes = [w[1][:] for w in w3q]

        def put_claims(c, tag=None):
            y = second_stage(c, w4_codes, w4_planes, zq, None, tag)
            nc.vector.tensor_tensor(pages[c][:].indirect(l_offs4[:]), y[:], wg2_t[:], ALU.mult)

        def put_lines(hf, hq, c, tag=None):
            y = second_stage(c, w3_codes, w3_planes, hq, d_t[:, c : c + 1], tag)
            nc.vector.tensor_tensor(
                pages[c][:].indirect(l_offs3[:, LIST_COLS * hf : LIST_COLS * (hf + 1)]),
                y[:],
                wg1_t[:, hf * COLS : (hf + 1) * COLS],
                ALU.mult,
            )

        put_claims(0)
        put_claims(1)
        hq0 = quantise_lines(0)
        put_claims(2, "late")
        put_lines(0, hq0, 0)
        put_lines(0, hq0, 1)
        hq1 = quantise_lines(1)
        put_lines(0, hq0, 2, "later")
        for c in range(PAGES):
            put_lines(1, hq1, c)
        for c in range(PAGES):
            for side in range(2):
                cols = slice(side * T2 // 2, (side + 1) * T2 // 2)
                nc.sync.dma_start(out[c * P : (c + 1) * P, cols], pages[c][:, cols])
